import numpy as np
import ml_dtypes


def mxq(x, axis, fmt="e4m3"):
    dtype, down = {"e4m3": (ml_dtypes.float8_e4m3fn, 7), "e5m2": (ml_dtypes.float8_e5m2, 14)}[fmt]
    v = np.moveaxis(np.asarray(x, np.float32).astype(ml_dtypes.bfloat16).astype(np.float64), axis, -1)
    blocks = v.reshape(v.shape[:-1] + (-1, 32))
    amax = np.abs(blocks).max(-1, keepdims=True)
    byte = np.maximum(np.where(amax > 0, np.frexp(amax)[1] - 1 + 127, 0) - down, 1)
    scale = np.exp2(byte - 127.0)
    codes = (blocks / scale).astype(np.float32).astype(dtype).astype(np.float64)
    return np.moveaxis((codes * scale).reshape(v.shape), -1, axis)


WIDE = False


def mx_kscale(k):
    if not WIDE:
        return np.ones(k)
    levels = np.array([10, -10, 5, -5, 0])
    if k % 512:
        return np.exp2(np.random.permutation(np.resize(levels, k // 32))).repeat(32)
    a = np.empty((k // 512, 16))
    for p in range(k // 512):
        a[p, :8] = np.random.permutation(np.resize(levels, 8))
        for g in range(8):
            far = levels[np.abs(levels - a[p, g]) >= 10]
            a[p, g + 8] = far[np.random.randint(len(far))]
    return np.exp2(a.ravel()).repeat(32)


def f64(x):
    return np.asarray(x).astype(np.float64)


def striped(idx):
    return np.tile(idx.reshape(-1, 16).T, (8, 1)).astype(np.uint16)


def unstriped(offs):
    return offs[:16].T.reshape(-1).astype(np.int64)


E2M1 = np.array([0.0, 0.5, 1.0, 1.5, 2.0, 3.0, 4.0, 6.0, -0.0, -0.5, -1.0, -1.5, -2.0, -3.0, -4.0, -6.0])


def pack_weight(w, fmt):
    k, n = w.shape
    w = f64(np.asarray(w, np.float32).astype(ml_dtypes.bfloat16)).reshape(k // 32, 32, n)
    amax = np.abs(w).max(1)
    if fmt == "e4m3":
        byte = np.frexp(amax)[1] - 1 + 127 - 7
    else:
        mant, ex = np.frexp(amax / 6.0)
        byte = np.where(mant > 0.5, ex, ex - 1) + 127
    byte = np.clip(np.where(amax > 0, byte, 1), 1, 254)
    scaled = (w * np.exp2(127.0 - byte)[:, None, :]).reshape(k, n).astype(np.float32)
    by_word = np.ascontiguousarray(scaled.reshape(k // 512, 128, 4, n).transpose(0, 1, 3, 2))
    if fmt == "e4m3":
        words = by_word.astype(ml_dtypes.float8_e4m3fn).view(np.uint8)
    else:
        c = by_word.astype(ml_dtypes.float4_e2m1fn).view(np.uint8) & 0xF
        words = (c[..., 0::2] | (c[..., 1::2] << 4)).reshape(k // 512, 128, 2 * n)
    return np.ascontiguousarray(words), np.ascontiguousarray(byte.astype(np.uint8).reshape(k // 512, 16, n))


def unpack_weight(words, scales, fmt):
    g, _, n = scales.shape
    words = np.ascontiguousarray(words).reshape(g, 128, n, -1)
    if fmt == "e4m3":
        vals = words.view(ml_dtypes.float8_e4m3fn).astype(np.float64)
    else:
        nib = np.empty((g, 128, n, 4), np.uint8)
        nib[..., 0::2] = words & 0xF
        nib[..., 1::2] = words >> 4
        vals = E2M1[nib]
    vals = vals * np.repeat(np.exp2(scales.astype(np.float64) - 127.0), 8, axis=1)[..., None]
    return vals.transpose(0, 1, 3, 2).reshape(g * 512, n)


def silu(v):
    return v / (1.0 + np.exp(-np.maximum(v, -700.0)))


K, T, E, C, N = 2560, 768, 2, 256, 128


def by_expert(wq, xq):
    return np.concatenate([wq[e].T @ xq[:, e * C:(e + 1) * C] for e in range(E)], axis=1)


def setup_inputs():
    n = np.random.standard_normal
    s = mx_kscale(K)[:, None]
    w = [pack_weight(m, "e2m1") for m in n((E + 1, K, N)) / np.sqrt(K) / s[None]]
    return {
        "xT": (n((K, T)) * s).astype(np.float32),
        "w_words": np.stack([m[0] for m in w]),
        "w_scales": np.stack([m[1] for m in w]),
        "b": (0.3 * n((N, E + 1))).astype(np.float32),
        "gate": np.tile(np.random.uniform(0.2, 1.0, E * C), (N, 1)).astype(np.float32),
        "offs": striped(np.random.permutation(T)[:E * C]),
    }


def reference(xT, w_words, w_scales, b, gate, offs):
    idx = unstriped(offs)
    w = np.stack([unpack_weight(w_words[e], w_scales[e], "e2m1") for e in range(E + 1)])
    wq = w
    xs = mxq(f64(xT), 0, "e4m3")
    ys = silu((wq[E].T @ xs) + f64(b)[:, E:])
    xq = mxq(f64(xT)[:, idx], 0, "e4m3")
    y = by_expert(w, xq)
    y = silu(y + np.repeat(f64(b)[:, :E], C, axis=1))
    out = ys
    out[:, idx] += f64(gate) * y
    return out

@@ -1,0 +1,198 @@
+from contextlib import ExitStack
+
+import concourse.mybir as mybir
+
+F32 = mybir.dt.float32
+BF16 = mybir.dt.bfloat16
+I32 = mybir.dt.int32
+U32 = mybir.dt.uint32
+U16 = mybir.dt.uint16
+U8 = mybir.dt.uint8
+FP8X4 = mybir.dt.float8_e4m3fn_x4
+FP4X4 = mybir.dt.float4_e2m1fn_x4
+SILU = mybir.ActivationFunctionType.Silu
+MULT = mybir.AluOpType.mult
+
+K, T, E, C, N = 2560, 768, 2, 256, 128
+S = E * C
+P = 128
+PASSES = K // 512
+FLOPS = 2 * K * N * (S + T)
+
+
+def tile_moe_shr_lin_silu_kernel(tc, xT, w_words, w_scales, b, gate, offs, out):
+    nc = tc.nc
+    with ExitStack() as ctx:
+        keep = ctx.enter_context(tc.tile_pool(name="keep", bufs=1))
+        psum = ctx.enter_context(tc.psum_pool(name="psum", bufs=1))
+
+        offs_sb = keep.tile([P, S // 16], U16, name="offs_sb")
+        nc.sync.dma_start(offs_sb[:], offs)
+
+        x_view = xT.rearrange("(a p j) t -> a p j t", p=P, j=4)
+        raw = [keep.tile([P, 2, T], F32, name=f"raw{u}") for u in range(2 * PASSES)]
+
+        def load(u, cols):
+            a, h = divmod(u, 2)
+            nc.sync.dma_start(raw[u][:, :, cols], x_view[a, :, 2 * h : 2 * h + 2, cols])
+
+        half0, half1, full = slice(0, T // 2), slice(T // 2, T), slice(0, T)
+        for u in range(2):
+            load(u, half0)
+            load(u, half1)
+        for u in range(2, 2 * PASSES):
+            load(u, full)
+
+        b_sb = keep.tile([P, E + 1], F32, name="b_sb")
+        nc.scalar.dma_start(b_sb[:], b)
+        wsc = keep.tile([P, 3 * PASSES, N], U8, align_bytes=64, name="wsc")
+        nc.gpsimd.memset(wsc[:].rearrange("p g n -> p (g n)").bitcast(I32), 0)
+        win = keep.tile([P, T], F32, name="win")
+        nc.gpsimd.memset(win[:], 0.0)
+        warm = keep.tile([P, 1], F32, name="warm")
+        warm_out = keep.tile([P, 1], F32, name="warm_out")
+        nc.gpsimd.memset(warm[:], 0.0)
+        nc.scalar.activation(warm_out[:], warm[:], SILU)
+
+        wq = keep.tile([P, 3 * PASSES, 2 * N], U8, align_bytes=64, name="wq")
+        nc.sync.dma_start(wq[:].bitcast(I32), w_words.bitcast(I32).rearrange("e a p n -> p (e a) n"))
+        ws_view = w_scales.bitcast(I32).rearrange("e a q n -> q (e a) n")
+        for q in range(4):
+            nc.sync.dma_start(wsc[32 * q : 32 * q + 4, :, :].bitcast(I32), ws_view[4 * q : 4 * q + 4, :, :])
+        gate_sb = keep.tile([P, S], F32, name="gate_sb")
+        nc.sync.dma_start(gate_sb[:], gate)
+
+        planes = [keep.tile([P, 2, 2 * T], BF16, align_bytes=64, name=f"planes{a}") for a in range(PASSES)]
+        gath = [keep.tile([P, 2, 2 * S], BF16, align_bytes=64, name=f"gath{a}") for a in range(PASSES)]
+        rin = [keep.tile([P, 4 * S], BF16, align_bytes=64, name=f"rin{a}") for a in range(PASSES)]
+        sin_ = [keep.tile([P, 4 * T], BF16, align_bytes=64, name=f"sin{a}") for a in range(PASSES)]
+        rcode = [keep.tile([P, S], U32, align_bytes=64, name=f"rcode{a}") for a in range(PASSES)]
+        rscale = [keep.tile([P, S], U8, align_bytes=64, name=f"rscale{a}") for a in range(PASSES)]
+        scode = [keep.tile([P, T], U32, align_bytes=64, name=f"scode{a}") for a in range(PASSES)]
+        sscale = [keep.tile([P, T], U8, align_bytes=64, name=f"sscale{a}") for a in range(PASSES)]
+
+        def cast(engine, u, cols):
+            a, h = divmod(u, 2)
+            dst = planes[a][:, h, :].rearrange("p (t e) -> p t e", e=2)[:, cols, :]
+            src = raw[u][:, :, cols].rearrange("p e t -> p t e")
+            if engine is nc.scalar:
+                nc.scalar.copy(dst, src)
+            else:
+                nc.vector.tensor_copy(dst, src)
+
+        def gather(u):
+            a, h = divmod(u, 2)
+            nc.vector.tensor_copy(gath[a][:, h, :].bitcast(U32), planes[a][:, h, :].bitcast(U32).indirect(offs_sb[:]))
+
+        def zip_pairs(engine, dst_tile, src_tile):
+            if engine is nc.scalar:
+                nc.scalar.copy(
+                    dst_tile[:].bitcast(F32).rearrange("p (t h) -> p t h", h=2),
+                    src_tile[:].bitcast(F32).rearrange("p h t -> p t h"),
+                )
+            else:
+                nc.vector.tensor_copy(
+                    dst_tile[:].rearrange("p (t h e) -> p t h e", h=2, e=2),
+                    src_tile[:].rearrange("p h (t e) -> p t h e", e=2),
+                )
+
+        def quant(code, scale, src, c0, c1):
+            nc.vector.quantize_mx(out=code[:, c0:c1].bitcast(FP8X4), scales=scale[:, c0:c1], in_=src[:, 4 * c0 : 4 * c1])
+
+        def quant_r(a):
+            quant(rcode[a], rscale[a], rin[a], 0, S)
+
+        def quant_s(a):
+            quant(scode[a], sscale[a], sin_[a], 0, 512)
+            quant(scode[a], sscale[a], sin_[a], 512, T)
+
+        groups_r = [(e, 128 * g, 128) for e in range(E) for g in (2 * e, 2 * e + 1)]
+        groups_s = [(E, 0, 512), (E, 512, 128), (E, 640, 128)]
+        acc_r = [psum.tile([P, 128], F32, name=f"acc_r{i}") for i in range(4)]
+        acc_s = [psum.tile([P, w], F32, name=f"acc_s{i}") for i, (e, c, w) in enumerate(groups_s)]
+
+        def mm(acc, e, a, code, scale, c, w):
+            nc.tensor.matmul_mx(
+                out=acc[:],
+                lhsT=wq[:, e * PASSES + a, :].bitcast(FP4X4),
+                lhsT_scale=wsc[:, e * PASSES + a, :],
+                rhs=code[:, c : c + w].bitcast(FP8X4),
+                rhs_scale=scale[:, c : c + w],
+                start=(a == 0),
+                stop=(a == PASSES - 1),
+            )
+
+        def mm_r(a):
+            for i, (e, c, w) in enumerate(groups_r):
+                mm(acc_r[i], e, a, rcode[a], rscale[a], c, w)
+
+        def mm_s(a):
+            for i, (e, c, w) in enumerate(groups_s):
+                mm(acc_s[i], e, a, scode[a], sscale[a], c, w)
+
+        V, A = nc.vector, nc.scalar
+        cast(A, 0, half0)
+        cast(V, 0, half1)
+        gather(0)
+        cast(A, 1, half0)
+        cast(V, 1, half1)
+        gather(1)
+        for u in range(2, 6):
+            cast(A, u, full)
+        zip_pairs(V, sin_[0], planes[0])
+        zip_pairs(V, rin[0], gath[0])
+        quant_s(0)
+        quant_r(0)
+        mm_s(0)
+        mm_r(0)
+        gather(2)
+        gather(3)
+        for u in range(6, 10):
+            cast(A, u, full)
+        zip_pairs(V, sin_[1], planes[1])
+        zip_pairs(V, rin[1], gath[1])
+        quant_s(1)
+        quant_r(1)
+        mm_s(1)
+        mm_r(1)
+        gather(4)
+        gather(5)
+        zip_pairs(V, rin[2], gath[2])
+        gather(6)
+        quant_r(2)
+        mm_r(2)
+        gather(7)
+        zip_pairs(A, sin_[2], planes[2])
+        zip_pairs(A, rin[3], gath[3])
+        gather(8)
+        gather(9)
+        zip_pairs(A, sin_[3], planes[3])
+        zip_pairs(A, rin[4], gath[4])
+        quant_s(2)
+        quant_r(3)
+        mm_s(2)
+        mm_r(3)
+        zip_pairs(A, sin_[4], planes[4])
+        quant_s(3)
+        quant_r(4)
+        mm_s(3)
+        mm_r(4)
+        y = keep.tile([P, S], F32, name="y")
+        for i, (e, c, w) in enumerate(groups_r):
+            nc.scalar.activation(y[:, c : c + w], acc_r[i][:], SILU, bias=b_sb[:, e : e + 1])
+        quant_s(4)
+        mm_s(4)
+        for e in range(E):
+            nc.vector.tensor_tensor(
+                win[:].indirect(offs_sb[:, e * C // 16 : (e + 1) * C // 16]),
+                y[:, e * C : (e + 1) * C],
+                gate_sb[:, e * C : (e + 1) * C],
+                MULT,
+            )
+        ys = keep.tile([P, T], F32, name="ys")
+        for i, (e, c, w) in enumerate(groups_s):
+            nc.scalar.activation(ys[:, c : c + w], acc_s[i][:], SILU, bias=b_sb[:, e : e + 1])
+        res = keep.tile([P, T], F32, name="res")
+        for cols in (half0, half1):
+            nc.vector.tensor_add(res[:, cols], ys[:, cols], win[:, cols])
+            nc.sync.dma_start(out[:, cols], res[:, cols])

@@ -12,6 +12,7 @@ FP8X4 = mybir.dt.float8_e4m3fn_x4
 FP4X4 = mybir.dt.float4_e2m1fn_x4
 SILU = mybir.ActivationFunctionType.Silu
 MULT = mybir.AluOpType.mult
+ADD = mybir.AluOpType.add
 
 K, T, E, C, N = 2560, 768, 2, 256, 128
 S = E * C
@@ -26,9 +27,6 @@ def tile_moe_shr_lin_silu_kernel(tc, xT, w_words, w_scales, b, gate, offs, out):
         keep = ctx.enter_context(tc.tile_pool(name="keep", bufs=1))
         psum = ctx.enter_context(tc.psum_pool(name="psum", bufs=1))
 
-        offs_sb = keep.tile([P, S // 16], U16, name="offs_sb")
-        nc.sync.dma_start(offs_sb[:], offs)
-
         x_view = xT.rearrange("(a p j) t -> a p j t", p=P, j=4)
         raw = [keep.tile([P, 2, T], F32, name=f"raw{u}") for u in range(2 * PASSES)]
 
@@ -36,10 +34,14 @@ def tile_moe_shr_lin_silu_kernel(tc, xT, w_words, w_scales, b, gate, offs, out):
             a, h = divmod(u, 2)
             nc.sync.dma_start(raw[u][:, :, cols], x_view[a, :, 2 * h : 2 * h + 2, cols])
 
-        half0, half1, full = slice(0, T // 2), slice(T // 2, T), slice(0, T)
-        for u in range(2):
-            load(u, half0)
-            load(u, half1)
+        CUT = T // 2
+        half0, half1, full = slice(0, CUT), slice(CUT, T), slice(0, T)
+        offs_sb = keep.tile([P, S // 16], U16, name="offs_sb")
+        load(0, half0)
+        nc.sync.dma_start(offs_sb[:], offs)
+        load(0, half1)
+        load(1, half0)
+        load(1, half1)
         for u in range(2, 2 * PASSES):
             load(u, full)
 
@@ -51,7 +53,7 @@ def tile_moe_shr_lin_silu_kernel(tc, xT, w_words, w_scales, b, gate, offs, out):
         nc.gpsimd.memset(win[:], 0.0)
         warm = keep.tile([P, 1], F32, name="warm")
         warm_out = keep.tile([P, 1], F32, name="warm_out")
-        nc.gpsimd.memset(warm[:], 0.0)
+        nc.vector.memset(warm[:], 0.0)
         nc.scalar.activation(warm_out[:], warm[:], SILU)
 
         wq = keep.tile([P, 3 * PASSES, 2 * N], U8, align_bytes=64, name="wq")
@@ -64,12 +66,12 @@ def tile_moe_shr_lin_silu_kernel(tc, xT, w_words, w_scales, b, gate, offs, out):
 
         planes = [keep.tile([P, 2, 2 * T], BF16, align_bytes=64, name=f"planes{a}") for a in range(PASSES)]
         gath = [keep.tile([P, 2, 2 * S], BF16, align_bytes=64, name=f"gath{a}") for a in range(PASSES)]
-        rin = [keep.tile([P, 4 * S], BF16, align_bytes=64, name=f"rin{a}") for a in range(PASSES)]
-        sin_ = [keep.tile([P, 4 * T], BF16, align_bytes=64, name=f"sin{a}") for a in range(PASSES)]
-        rcode = [keep.tile([P, S], U32, align_bytes=64, name=f"rcode{a}") for a in range(PASSES)]
-        rscale = [keep.tile([P, S], U8, align_bytes=64, name=f"rscale{a}") for a in range(PASSES)]
-        scode = [keep.tile([P, T], U32, align_bytes=64, name=f"scode{a}") for a in range(PASSES)]
-        sscale = [keep.tile([P, T], U8, align_bytes=64, name=f"sscale{a}") for a in range(PASSES)]
+        rin = keep.tile([P, PASSES * 4 * S], BF16, align_bytes=64, name="rin")
+        sin_ = keep.tile([P, PASSES * 4 * T], BF16, align_bytes=64, name="sin")
+        rcode = keep.tile([P, PASSES * S], U32, align_bytes=64, name="rcode")
+        rscale = keep.tile([P, PASSES * S], U8, align_bytes=64, name="rscale")
+        scode = keep.tile([P, PASSES * T], U32, align_bytes=64, name="scode")
+        sscale = keep.tile([P, PASSES * T], U8, align_bytes=64, name="sscale")
 
         def cast(engine, u, cols):
             a, h = divmod(u, 2)
@@ -77,122 +79,126 @@ def tile_moe_shr_lin_silu_kernel(tc, xT, w_words, w_scales, b, gate, offs, out):
             src = raw[u][:, :, cols].rearrange("p e t -> p t e")
             if engine is nc.scalar:
                 nc.scalar.copy(dst, src)
-            else:
+            elif engine is nc.vector:
                 nc.vector.tensor_copy(dst, src)
+            else:
+                nc.gpsimd.tensor_scalar(dst, src, 1.0, 0.0, MULT, ADD)
 
         def gather(u):
             a, h = divmod(u, 2)
             nc.vector.tensor_copy(gath[a][:, h, :].bitcast(U32), planes[a][:, h, :].bitcast(U32).indirect(offs_sb[:]))
 
-        def zip_pairs(engine, dst_tile, src_tile):
+        def zip_pairs(engine, dst, src):
             if engine is nc.scalar:
                 nc.scalar.copy(
-                    dst_tile[:].bitcast(F32).rearrange("p (t h) -> p t h", h=2),
-                    src_tile[:].bitcast(F32).rearrange("p h t -> p t h"),
+                    dst.bitcast(F32).rearrange("p (t h) -> p t h", h=2),
+                    src[:].bitcast(F32).rearrange("p h t -> p t h"),
                 )
             else:
                 nc.vector.tensor_copy(
-                    dst_tile[:].rearrange("p (t h e) -> p t h e", h=2, e=2),
-                    src_tile[:].rearrange("p h (t e) -> p t h e", e=2),
+                    dst.rearrange("p (t h e) -> p t h e", h=2, e=2),
+                    src[:].rearrange("p h (t e) -> p t h e", e=2),
                 )
+
+        def zip_s(engine, a):
+            zip_pairs(engine, sin_[:, 4 * T * a : 4 * T * (a + 1)], planes[a])
+
+        def zip_r(engine, a):
+            zip_pairs(engine, rin[:, 4 * S * a : 4 * S * (a + 1)], gath[a])
 
         def quant(code, scale, src, c0, c1):
             nc.vector.quantize_mx(out=code[:, c0:c1].bitcast(FP8X4), scales=scale[:, c0:c1], in_=src[:, 4 * c0 : 4 * c1])
 
-        def quant_r(a):
-            quant(rcode[a], rscale[a], rin[a], 0, S)
+        def quant_r(c0, c1):
+            quant(rcode, rscale, rin, c0, c1)
 
-        def quant_s(a):
-            quant(scode[a], sscale[a], sin_[a], 0, 512)
-            quant(scode[a], sscale[a], sin_[a], 512, T)
+        def quant_s(c0, c1):
+            quant(scode, sscale, sin_, c0, c1)
 
         groups_r = [(e, 128 * g, 128) for e in range(E) for g in (2 * e, 2 * e + 1)]
         groups_s = [(E, 0, 512), (E, 512, 128), (E, 640, 128)]
         acc_r = [psum.tile([P, 128], F32, name=f"acc_r{i}") for i in range(4)]
         acc_s = [psum.tile([P, w], F32, name=f"acc_s{i}") for i, (e, c, w) in enumerate(groups_s)]
 
-        def mm(acc, e, a, code, scale, c, w):
+        def mm(acc, e, a, code, scale, c, w, first, last):
             nc.tensor.matmul_mx(
                 out=acc[:],
                 lhsT=wq[:, e * PASSES + a, :].bitcast(FP4X4),
                 lhsT_scale=wsc[:, e * PASSES + a, :],
                 rhs=code[:, c : c + w].bitcast(FP8X4),
                 rhs_scale=scale[:, c : c + w],
-                start=(a == 0),
-                stop=(a == PASSES - 1),
+                start=first,
+                stop=last,
             )
 
-        def mm_r(a):
+        def mm_r(a, first=False, last=False):
             for i, (e, c, w) in enumerate(groups_r):
-                mm(acc_r[i], e, a, rcode[a], rscale[a], c, w)
+                mm(acc_r[i], e, a, rcode, rscale, S * a + c, w, first, last)
 
-        def mm_s(a):
+        def mm_s(a, first=False, last=False):
             for i, (e, c, w) in enumerate(groups_s):
-                mm(acc_s[i], e, a, scode[a], sscale[a], c, w)
+                mm(acc_s[i], e, a, scode, sscale, T * a + c, w, first, last)
 
-        V, A = nc.vector, nc.scalar
-        cast(A, 0, half0)
+        y = keep.tile([P, S], F32, name="y")
+        ys = keep.tile([P, T], F32, name="ys")
+        res = keep.tile([P, T], F32, name="res")
+        V, A, G = nc.vector, nc.scalar, nc.gpsimd
+
+        cast(V, 0, half0)
+        cast(A, 1, half0)
         cast(V, 0, half1)
         gather(0)
-        cast(A, 1, half0)
         cast(V, 1, half1)
         gather(1)
-        for u in range(2, 6):
-            cast(A, u, full)
-        zip_pairs(V, sin_[0], planes[0])
-        zip_pairs(V, rin[0], gath[0])
-        quant_s(0)
-        quant_r(0)
-        mm_s(0)
-        mm_r(0)
+        cast(A, 2, full)
+        zip_s(V, 0)
+        cast(A, 3, full)
+        zip_r(V, 0)
         gather(2)
         gather(3)
-        for u in range(6, 10):
-            cast(A, u, full)
-        zip_pairs(V, sin_[1], planes[1])
-        zip_pairs(V, rin[1], gath[1])
-        quant_s(1)
-        quant_r(1)
-        mm_s(1)
-        mm_r(1)
+        cast(A, 4, full)
+        zip_s(V, 1)
+        cast(A, 5, full)
+        quant_s(0, 1024)
+        mm_s(0, first=True, last=False)
+        zip_r(V, 1)
         gather(4)
+        cast(A, 6, full)
         gather(5)
-        zip_pairs(V, rin[2], gath[2])
+        quant_r(0, 1024)
+        mm_r(0, first=True, last=False)
+        mm_r(1, first=False, last=False)
+        cast(A, 7, full)
         gather(6)
-        quant_r(2)
-        mm_r(2)
+        cast(A, 8, full)
         gather(7)
-        zip_pairs(A, sin_[2], planes[2])
-        zip_pairs(A, rin[3], gath[3])
+        cast(A, 9, full)
         gather(8)
         gather(9)
-        zip_pairs(A, sin_[3], planes[3])
-        zip_pairs(A, rin[4], gath[4])
-        quant_s(2)
-        quant_r(3)
-        mm_s(2)
-        mm_r(3)
-        zip_pairs(A, sin_[4], planes[4])
-        quant_s(3)
-        quant_r(4)
-        mm_s(3)
-        mm_r(4)
-        y = keep.tile([P, S], F32, name="y")
+        zip_r(A, 2)
+        zip_r(A, 3)
+        zip_r(V, 4)
+        quant_r(2048, 2560)
+        mm_r(4, first=False, last=False)
+        zip_s(A, 2)
+        quant_r(1024, 2048)
+        mm_r(2, first=False, last=False)
+        mm_r(3, first=False, last=True)
+        zip_s(A, 3)
+        quant_s(1024, 2048)
+        mm_s(1, first=False, last=False)
+        zip_s(A, 4)
         for i, (e, c, w) in enumerate(groups_r):
             nc.scalar.activation(y[:, c : c + w], acc_r[i][:], SILU, bias=b_sb[:, e : e + 1])
-        quant_s(4)
-        mm_s(4)
-        for e in range(E):
-            nc.vector.tensor_tensor(
-                win[:].indirect(offs_sb[:, e * C // 16 : (e + 1) * C // 16]),
-                y[:, e * C : (e + 1) * C],
-                gate_sb[:, e * C : (e + 1) * C],
-                MULT,
-            )
-        ys = keep.tile([P, T], F32, name="ys")
+        quant_s(2048, 3072)
+        mm_s(2, first=False, last=False)
+        mm_s(3, first=False, last=False)
+        quant_s(3072, 3584)
+        quant_s(3584, 3840)
+        mm_s(4, first=False, last=True)
+        nc.vector.tensor_tensor(win[:].indirect(offs_sb[:]), y[:], gate_sb[:], MULT)
         for i, (e, c, w) in enumerate(groups_s):
             nc.scalar.activation(ys[:, c : c + w], acc_s[i][:], SILU, bias=b_sb[:, e : e + 1])
-        res = keep.tile([P, T], F32, name="res")
-        for cols in (half0, half1):
+        for cols in (slice(0, 512), slice(512, T)):
             nc.vector.tensor_add(res[:, cols], ys[:, cols], win[:, cols])
             nc.sync.dma_start(out[:, cols], res[:, cols])

from contextlib import ExitStack

import concourse.mybir as mybir

F32 = mybir.dt.float32
BF16 = mybir.dt.bfloat16
I32 = mybir.dt.int32
U32 = mybir.dt.uint32
U16 = mybir.dt.uint16
U8 = mybir.dt.uint8
FP8X4 = mybir.dt.float8_e4m3fn_x4
FP4X4 = mybir.dt.float4_e2m1fn_x4
SILU = mybir.ActivationFunctionType.Silu
MULT = mybir.AluOpType.mult
ADD = mybir.AluOpType.add

K, T, E, C, N = 2560, 768, 2, 256, 128
S = E * C
P = 128
PASSES = K // 512
FLOPS = 2 * K * N * (S + T)


def tile_moe_shr_lin_silu_kernel(tc, xT, w_words, w_scales, b, gate, offs, out):
    nc = tc.nc
    with ExitStack() as ctx:
        keep = ctx.enter_context(tc.tile_pool(name="keep", bufs=1))
        psum = ctx.enter_context(tc.psum_pool(name="psum", bufs=1))

        x_view = xT.rearrange("(a p j) t -> a p j t", p=P, j=4)
        raw = [keep.tile([P, 2, T], F32, name=f"raw{u}") for u in range(2 * PASSES)]

        def load(u, cols):
            a, h = divmod(u, 2)
            nc.sync.dma_start(raw[u][:, :, cols], x_view[a, :, 2 * h : 2 * h + 2, cols])

        CUT = T // 2
        half0, half1, full = slice(0, CUT), slice(CUT, T), slice(0, T)
        offs_sb = keep.tile([P, S // 16], U16, name="offs_sb")
        load(0, half0)
        nc.sync.dma_start(offs_sb[:], offs)
        load(0, half1)
        load(1, half0)
        load(1, half1)
        for u in range(2, 2 * PASSES):
            load(u, full)

        b_sb = keep.tile([P, E + 1], F32, name="b_sb")
        nc.scalar.dma_start(b_sb[:], b)
        wsc = keep.tile([P, 3 * PASSES, N], U8, align_bytes=64, name="wsc")
        nc.gpsimd.memset(wsc[:].rearrange("p g n -> p (g n)").bitcast(I32), 0)
        win = keep.tile([P, T], F32, name="win")
        nc.gpsimd.memset(win[:], 0.0)
        warm = keep.tile([P, 1], F32, name="warm")
        warm_out = keep.tile([P, 1], F32, name="warm_out")
        nc.vector.memset(warm[:], 0.0)
        nc.scalar.activation(warm_out[:], warm[:], SILU)

        wq = keep.tile([P, 3 * PASSES, 2 * N], U8, align_bytes=64, name="wq")
        nc.sync.dma_start(wq[:].bitcast(I32), w_words.bitcast(I32).rearrange("e a p n -> p (e a) n"))
        ws_view = w_scales.bitcast(I32).rearrange("e a q n -> q (e a) n")
        for q in range(4):
            nc.sync.dma_start(wsc[32 * q : 32 * q + 4, :, :].bitcast(I32), ws_view[4 * q : 4 * q + 4, :, :])
        gate_sb = keep.tile([P, S], F32, name="gate_sb")
        nc.sync.dma_start(gate_sb[:], gate)

        planes = [keep.tile([P, 2, 2 * T], BF16, align_bytes=64, name=f"planes{a}") for a in range(PASSES)]
        gath = [keep.tile([P, 2, 2 * S], BF16, align_bytes=64, name=f"gath{a}") for a in range(PASSES)]
        rin = keep.tile([P, PASSES * 4 * S], BF16, align_bytes=64, name="rin")
        sin_ = keep.tile([P, PASSES * 4 * T], BF16, align_bytes=64, name="sin")
        rcode = keep.tile([P, PASSES * S], U32, align_bytes=64, name="rcode")
        rscale = keep.tile([P, PASSES * S], U8, align_bytes=64, name="rscale")
        scode = keep.tile([P, PASSES * T], U32, align_bytes=64, name="scode")
        sscale = keep.tile([P, PASSES * T], U8, align_bytes=64, name="sscale")

        def cast(engine, u, cols):
            a, h = divmod(u, 2)
            dst = planes[a][:, h, :].rearrange("p (t e) -> p t e", e=2)[:, cols, :]
            src = raw[u][:, :, cols].rearrange("p e t -> p t e")
            if engine is nc.scalar:
                nc.scalar.copy(dst, src)
            elif engine is nc.vector:
                nc.vector.tensor_copy(dst, src)
            else:
                nc.gpsimd.tensor_scalar(dst, src, 1.0, 0.0, MULT, ADD)

        def gather(u):
            a, h = divmod(u, 2)
            nc.vector.tensor_copy(gath[a][:, h, :].bitcast(U32), planes[a][:, h, :].bitcast(U32).indirect(offs_sb[:]))

        def zip_pairs(engine, dst, src):
            if engine is nc.scalar:
                nc.scalar.copy(
                    dst.bitcast(F32).rearrange("p (t h) -> p t h", h=2),
                    src[:].bitcast(F32).rearrange("p h t -> p t h"),
                )
            else:
                nc.vector.tensor_copy(
                    dst.rearrange("p (t h e) -> p t h e", h=2, e=2),
                    src[:].rearrange("p h (t e) -> p t h e", e=2),
                )

        def zip_s(engine, a):
            zip_pairs(engine, sin_[:, 4 * T * a : 4 * T * (a + 1)], planes[a])

        def zip_r(engine, a):
            zip_pairs(engine, rin[:, 4 * S * a : 4 * S * (a + 1)], gath[a])

        def quant(code, scale, src, c0, c1):
            nc.vector.quantize_mx(out=code[:, c0:c1].bitcast(FP8X4), scales=scale[:, c0:c1], in_=src[:, 4 * c0 : 4 * c1])

        def quant_r(c0, c1):
            quant(rcode, rscale, rin, c0, c1)

        def quant_s(c0, c1):
            quant(scode, sscale, sin_, c0, c1)

        groups_r = [(e, 128 * g, 128) for e in range(E) for g in (2 * e, 2 * e + 1)]
        groups_s = [(E, 0, 512), (E, 512, 128), (E, 640, 128)]
        acc_r = [psum.tile([P, 128], F32, name=f"acc_r{i}") for i in range(4)]
        acc_s = [psum.tile([P, w], F32, name=f"acc_s{i}") for i, (e, c, w) in enumerate(groups_s)]

        def mm(acc, e, a, code, scale, c, w, first, last):
            nc.tensor.matmul_mx(
                out=acc[:],
                lhsT=wq[:, e * PASSES + a, :].bitcast(FP4X4),
                lhsT_scale=wsc[:, e * PASSES + a, :],
                rhs=code[:, c : c + w].bitcast(FP8X4),
                rhs_scale=scale[:, c : c + w],
                start=first,
                stop=last,
            )

        def mm_r(a, first=False, last=False):
            for i, (e, c, w) in enumerate(groups_r):
                mm(acc_r[i], e, a, rcode, rscale, S * a + c, w, first, last)

        def mm_s(a, first=False, last=False):
            for i, (e, c, w) in enumerate(groups_s):
                mm(acc_s[i], e, a, scode, sscale, T * a + c, w, first, last)

        y = keep.tile([P, S], F32, name="y")
        ys = keep.tile([P, T], F32, name="ys")
        res = keep.tile([P, T], F32, name="res")
        V, A, G = nc.vector, nc.scalar, nc.gpsimd

        cast(V, 0, half0)
        cast(A, 1, half0)
        cast(V, 0, half1)
        gather(0)
        cast(V, 1, half1)
        gather(1)
        cast(A, 2, full)
        zip_s(V, 0)
        cast(A, 3, full)
        zip_r(V, 0)
        gather(2)
        gather(3)
        cast(A, 4, full)
        zip_s(V, 1)
        cast(A, 5, full)
        quant_s(0, 1024)
        mm_s(0, first=True, last=False)
        zip_r(V, 1)
        gather(4)
        cast(A, 6, full)
        gather(5)
        quant_r(0, 1024)
        mm_r(0, first=True, last=False)
        mm_r(1, first=False, last=False)
        cast(A, 7, full)
        gather(6)
        cast(A, 8, full)
        gather(7)
        cast(A, 9, full)
        gather(8)
        gather(9)
        zip_r(A, 2)
        zip_r(A, 3)
        zip_r(V, 4)
        quant_r(2048, 2560)
        mm_r(4, first=False, last=False)
        zip_s(A, 2)
        quant_r(1024, 2048)
        mm_r(2, first=False, last=False)
        mm_r(3, first=False, last=True)
        zip_s(A, 3)
        quant_s(1024, 2048)
        mm_s(1, first=False, last=False)
        zip_s(A, 4)
        for i, (e, c, w) in enumerate(groups_r):
            nc.scalar.activation(y[:, c : c + w], acc_r[i][:], SILU, bias=b_sb[:, e : e + 1])
        quant_s(2048, 3072)
        mm_s(2, first=False, last=False)
        mm_s(3, first=False, last=False)
        quant_s(3072, 3584)
        quant_s(3584, 3840)
        mm_s(4, first=False, last=True)
        nc.vector.tensor_tensor(win[:].indirect(offs_sb[:]), y[:], gate_sb[:], MULT)
        for i, (e, c, w) in enumerate(groups_s):
            nc.scalar.activation(ys[:, c : c + w], acc_s[i][:], SILU, bias=b_sb[:, e : e + 1])
        for cols in (slice(0, 512), slice(512, T)):
            nc.vector.tensor_add(res[:, cols], ys[:, cols], win[:, cols])
            nc.sync.dma_start(out[:, cols], res[:, cols])
